import numpy as np
import ml_dtypes


def mxq(x, axis, fmt="e4m3"):
    dtype, down = {"e4m3": (ml_dtypes.float8_e4m3fn, 7), "e5m2": (ml_dtypes.float8_e5m2, 14)}[fmt]
    v = np.moveaxis(np.asarray(x, np.float32).astype(ml_dtypes.bfloat16).astype(np.float64), axis, -1)
    blocks = v.reshape(v.shape[:-1] + (-1, 32))
    amax = np.abs(blocks).max(-1, keepdims=True)
    byte = np.maximum(np.where(amax > 0, np.frexp(amax)[1] - 1 + 127, 0) - down, 1)
    scale = np.exp2(byte - 127.0)
    codes = (blocks / scale).astype(np.float32).astype(dtype).astype(np.float64)
    return np.moveaxis((codes * scale).reshape(v.shape), -1, axis)


WIDE = False


def mx_kscale(k):
    if not WIDE:
        return np.ones(k)
    levels = np.array([10, -10, 5, -5, 0])
    if k % 512:
        return np.exp2(np.random.permutation(np.resize(levels, k // 32))).repeat(32)
    a = np.empty((k // 512, 16))
    for p in range(k // 512):
        a[p, :8] = np.random.permutation(np.resize(levels, 8))
        for g in range(8):
            far = levels[np.abs(levels - a[p, g]) >= 10]
            a[p, g + 8] = far[np.random.randint(len(far))]
    return np.exp2(a.ravel()).repeat(32)


def f64(x):
    return np.asarray(x).astype(np.float64)


def striped(idx):
    return np.tile(idx.reshape(-1, 16).T, (8, 1)).astype(np.uint16)


def unstriped(offs):
    return offs[:16].T.reshape(-1).astype(np.int64)


E2M1 = np.array([0.0, 0.5, 1.0, 1.5, 2.0, 3.0, 4.0, 6.0, -0.0, -0.5, -1.0, -1.5, -2.0, -3.0, -4.0, -6.0])


def pack_weight(w, fmt):
    k, n = w.shape
    w = f64(np.asarray(w, np.float32).astype(ml_dtypes.bfloat16)).reshape(k // 32, 32, n)
    amax = np.abs(w).max(1)
    if fmt == "e4m3":
        byte = np.frexp(amax)[1] - 1 + 127 - 7
    else:
        mant, ex = np.frexp(amax / 6.0)
        byte = np.where(mant > 0.5, ex, ex - 1) + 127
    byte = np.clip(np.where(amax > 0, byte, 1), 1, 254)
    scaled = (w * np.exp2(127.0 - byte)[:, None, :]).reshape(k, n).astype(np.float32)
    by_word = np.ascontiguousarray(scaled.reshape(k // 512, 128, 4, n).transpose(0, 1, 3, 2))
    if fmt == "e4m3":
        words = by_word.astype(ml_dtypes.float8_e4m3fn).view(np.uint8)
    else:
        c = by_word.astype(ml_dtypes.float4_e2m1fn).view(np.uint8) & 0xF
        words = (c[..., 0::2] | (c[..., 1::2] << 4)).reshape(k // 512, 128, 2 * n)
    return np.ascontiguousarray(words), np.ascontiguousarray(byte.astype(np.uint8).reshape(k // 512, 16, n))


def unpack_weight(words, scales, fmt):
    g, _, n = scales.shape
    words = np.ascontiguousarray(words).reshape(g, 128, n, -1)
    if fmt == "e4m3":
        vals = words.view(ml_dtypes.float8_e4m3fn).astype(np.float64)
    else:
        nib = np.empty((g, 128, n, 4), np.uint8)
        nib[..., 0::2] = words & 0xF
        nib[..., 1::2] = words >> 4
        vals = E2M1[nib]
    vals = vals * np.repeat(np.exp2(scales.astype(np.float64) - 127.0), 8, axis=1)[..., None]
    return vals.transpose(0, 1, 3, 2).reshape(g * 512, n)


def gelu(v):
    return 0.5 * v * (1.0 + np.tanh(np.sqrt(2.0 / np.pi) * (v + 0.044715 * v**3)))


def pack_table4(v):
    words, scales = pack_weight(v, "e2m1")
    g, t = words.shape[0] // 2, v.shape[1]
    words = words.reshape(g, 2, 128, t, 2).transpose(0, 2, 3, 1, 4)
    return np.concatenate([words.reshape(g, -1), scales.reshape(g, -1)], axis=1)


def unpack_table4(tab):
    g, t = tab.shape[0], tab.shape[1] // 544
    words = tab[:, :512 * t].reshape(g, 128, t, 2, 2).transpose(0, 3, 1, 2, 4).reshape(2 * g, 128, 2 * t)
    return unpack_weight(words, tab[:, 512 * t:].reshape(2 * g, 16, t), "e2m1")


K, T, S, H, N = 2048, 2048, 1024, 512, 512

def setup_inputs():
    n = np.random.standard_normal
    s = mx_kscale(K)[:, None]
    u = mx_kscale(H)[:, None]
    tab = pack_table4(n((K, T)) * s)
    wx = n((K, H)) / np.sqrt(K) / s * u.T
    wy = n((K, H)) / np.sqrt(K) / s * u.T
    w4_words, w4_scales = pack_weight(n((H, N)) / np.sqrt(H) / u, "e2m1")
    return {
        "tab": tab,
        "offs": striped(np.random.permutation(T)[:S]),
        "wx": wx.astype(np.float32),
        "wy": wy.astype(np.float32),
        "w4_words": w4_words,
        "w4_scales": w4_scales,
        "bias": (0.5 * n(N)).astype(np.float32),
    }

def reference(tab, offs, wx, wy, w4_words, w4_scales, bias):
    v = unpack_table4(tab)[:, unstriped(offs)]
    gx = mxq(f64(wx), 0, "e4m3").T @ v
    gy = mxq(f64(wy), 0, "e4m3").T @ v
    h = np.sqrt(np.square(gx) + np.square(gy))
    hq = mxq(h, 0, "e4m3")
    w4 = unpack_weight(w4_words, w4_scales, "e2m1")
    return (w4.T @ hq) + f64(bias)[:, None]

@@ -1,0 +1,257 @@
+from contextlib import ExitStack
+
+import concourse.mybir as mybir
+
+K, T, S, H, N = 2048, 2048, 1024, 512, 512
+FLOPS = 2 * 2 * K * H * S + 2 * H * N * S
+
+F32 = mybir.dt.float32
+BF16 = mybir.dt.bfloat16
+I32 = mybir.dt.int32
+U32 = mybir.dt.uint32
+U16 = mybir.dt.uint16
+U8 = mybir.dt.uint8
+FP8X4 = mybir.dt.float8_e4m3fn_x4
+FP4X4 = mybir.dt.float4_e2m1fn_x4
+ACT = mybir.ActivationFunctionType
+ADD = mybir.AluOpType.add
+
+P = 128
+PACK = 4
+K_PASS = P * PACK
+PASSES = K // K_PASS
+HALF = 512
+HALVES = S // HALF
+QUARTER = 256
+QUARTERS = S // QUARTER
+
+
+def tile_list_face_gradient_magnitudes_kernel(tc, tab, offs, wx, wy, w4_words, w4_scales, bias, out):
+    nc = tc.nc
+    with ExitStack() as ctx:
+        keep = ctx.enter_context(tc.tile_pool(name="keep", bufs=1))
+        ring = ctx.enter_context(tc.tile_pool(name="ring", bufs=4))
+        psum = ctx.enter_context(tc.psum_pool(name="psum", bufs=1))
+
+        def held(shape, dtype, name):
+            return keep.tile(shape, dtype, name=name, align_bytes=64)
+
+        def streamed(shape, dtype, name):
+            return ring.tile(shape, dtype, name=name, tag="stream", align_bytes=64)
+
+        offsets = keep.tile([P, S // 16], U16, name="offsets")
+        nc.sync.dma_start(offsets[:], offs)
+
+        tab_scales = held([P, T], U8, "tab_scales")
+        for quad in range(4):
+            nc.vector.memset(tab_scales[32 * quad: 32 * quad + 16, :].bitcast(I32), 0)
+        zero_in = held([P, 1], F32, "zero_in")
+        nc.vector.memset(zero_in[:], 0.0)
+        moved = [held([P, S], U8, "moved%d" % a) for a in range(PASSES)]
+        for plane in moved:
+            nc.vector.memset(plane[:].bitcast(I32), 0)
+        w4_plane = held([P, N], U8, "w4_plane")
+        nc.gpsimd.memset(w4_plane[:], 0)
+
+        scale_rows = tab[:, 512 * T:].rearrange("m (h q t) -> m h q t", h=2, q=16)
+        for quad in range(4):
+            for m in range(2):
+                queue = nc.sync if quad == 0 else nc.scalar
+                queue.dma_start(
+                    tab_scales[32 * quad + 16 + 8 * m: 32 * quad + 24 + 8 * m, :].bitcast(I32),
+                    scale_rows[m, :, 4 * quad: 4 * quad + 4, :].bitcast(I32),
+                )
+        zero = held([P, 1], F32, "zero")
+        nc.scalar.activation(zero[:], zero_in[:], ACT.Sqrt)
+
+        def load_words(m):
+            words = streamed([P, T], I32, "words%d" % m)
+            nc.sync.dma_start(words[:], tab[m, : 512 * T].rearrange("(p b) -> p b", p=P).bitcast(I32))
+            return words
+
+        def load_weight(w, a, c0, c1, name):
+            raw = streamed([P, PACK, c1 - c0], F32, name)
+            rows = w[a * K_PASS: (a + 1) * K_PASS, c0:c1]
+            nc.sync.dma_start(raw[:], rows.rearrange("(p j) c -> p j c", j=PACK))
+            return raw
+
+        raw_x, raw_y, words = [], [], []
+        for a in range(PASSES):
+            if a == 2:
+                words.append(load_words(1))
+            raw_x.append(load_weight(wx, a, 0, H, "raw_x%d" % a))
+            if a == 0:
+                words.append(load_words(0))
+        for a in range(PASSES - 1):
+            raw_y.append(load_weight(wy, a, 0, H, "raw_y%d" % a))
+        last_a = load_weight(wy, PASSES - 1, 0, H // 2, "raw_y3a")
+        last_b = load_weight(wy, PASSES - 1, H // 2, H, "raw_y3b")
+
+        w4 = held([P, 2 * N], U8, "w4")
+        nc.gpsimd.dma_start(w4[:].bitcast(I32), w4_words[0].bitcast(I32))
+        for quad in range(4):
+            nc.gpsimd.dma_start(
+                w4_plane[32 * quad: 32 * quad + 4, :].bitcast(I32),
+                w4_scales[0, 4 * quad: 4 * quad + 4, :].bitcast(I32),
+            )
+        bias_sb = streamed([P, N // P], F32, "bias_sb")
+        with nc.allow_non_contiguous_dma(reason="one bias value for each partition and output tile"):
+            nc.sync.dma_start(bias_sb[:], bias.rearrange("(c p) -> p c", p=P))
+
+        picked_scales = held([P, S], U8, "picked_scales")
+        nc.vector.tensor_copy(picked_scales[:], tab_scales[:].indirect(offsets[:]))
+        for a in range(PASSES):
+            nc.scalar.dma_start(
+                moved[a][0:100, :].bitcast(I32),
+                picked_scales[16 + 4 * a: 116 + 4 * a, :].bitcast(I32),
+            )
+        planes = moved
+
+        parted = {}
+
+        def gather(m, hf):
+            picked = held([P, HALF], U32, "picked%d_%d" % (m, hf))
+            cols = slice(hf * HALF // 16, (hf + 1) * HALF // 16)
+            nc.vector.tensor_copy(picked[:], words[m][:].bitcast(U32).indirect(offsets[:, cols]))
+            part = held([P, 2, HALF], U16, "parted%d_%d" % (m, hf))
+            nc.vector.tensor_copy(part[:], picked[:].bitcast(U16).rearrange("p (s h) -> p h s", h=2))
+            parted[m, hf] = part
+
+        def cast(engine_copy, grouped, raw, m0, m1, base):
+            dst = grouped[:].rearrange("p (t m j) -> p m j t", t=PACK, j=PACK)[:, m0:m1]
+            src = raw[:].rearrange("p j (m t) -> p m j t", t=PACK)[:, m0 - base: m1 - base]
+            engine_copy(dst, src)
+
+        def new_grouped():
+            return ring.tile([P, PACK * H], BF16, name="grouped", align_bytes=64)
+
+        def quantise(grouped, name, pieces):
+            codes = held([P, H], U32, name + "_codes")
+            scales = held([P, H], U8, name + "_scales")
+            width = H // pieces
+            for i in range(pieces):
+                cols = slice(i * width, (i + 1) * width)
+                nc.vector.quantize_mx(
+                    out=codes[:, cols].bitcast(FP8X4),
+                    scales=scales[:, cols],
+                    in_=grouped[:, PACK * i * width: PACK * (i + 1) * width],
+                )
+            return codes, scales
+
+        def banks(hf):
+            return [psum.tile([P, HALF], F32, name="bank%d" % (4 * hf + t)) for t in range(PACK)]
+
+        def multiply(acc, weight, a, hf):
+            codes, scales = weight
+            for t in range(PACK):
+                cols = slice(t * P, (t + 1) * P)
+                nc.tensor.matmul_mx(
+                    out=acc[t][:],
+                    lhsT=codes[:, cols].bitcast(FP8X4),
+                    lhsT_scale=scales[:, cols],
+                    rhs=parted[a // 2, hf][:, a % 2, :].bitcast(FP4X4),
+                    rhs_scale=planes[a][:, hf * HALF: (hf + 1) * HALF],
+                    start=(a == 0),
+                    stop=(a == PASSES - 1),
+                )
+
+        gx = [banks(hf) for hf in range(HALVES)]
+        for a in range(PASSES):
+            grouped = new_grouped()
+            cast(nc.scalar.copy if a < PASSES - 1 else nc.vector.tensor_copy, grouped, raw_x[a], 0, P, 0)
+            if a % 2 == 0:
+                gather(a // 2, 0)
+            weight = quantise(grouped, "wx%d" % a, 1)
+            if a % 2 == 0:
+                gather(a // 2, 1)
+            for hf in range(HALVES):
+                multiply(gx[hf], weight, a, hf)
+
+        gx2 = []
+        for hf in range(HALVES):
+            sq = held([P, 2, PACK, QUARTER], F32, "gx2_%d" % hf)
+            for t in range(PACK):
+                nc.scalar.activation(
+                    sq[:, :, t, :], gx[hf][t][:].rearrange("p (q j) -> p q j", q=2), ACT.Square, bias=zero[:]
+                )
+            gx2.append(sq)
+
+        wy_q = []
+        for a in range(PASSES):
+            grouped = new_grouped()
+            if a < PASSES - 1:
+                cast(nc.vector.tensor_copy, grouped, raw_y[a], 0, P, 0)
+                wy_q.append(quantise(grouped, "wy%d" % a, 1))
+            else:
+                cast(nc.vector.tensor_copy, grouped, last_a, 0, 64, 0)
+                cast(nc.scalar.copy, grouped, last_b, 64, 84, 64)
+                cast(nc.vector.tensor_copy, grouped, last_b, 84, P, 64)
+                wy_q.append(quantise(grouped, "wy%d" % a, PACK))
+        gy = []
+        for hf in range(HALVES):
+            gy.append(banks(hf))
+            for a in range(PASSES):
+                multiply(gy[hf], wy_q[a], a, hf)
+
+        out_view = out.rearrange("(c p) j -> p c j", p=P)
+        total = {}
+        hq = {}
+
+        def square_add(q):
+            hf, side = divmod(q, 2)
+            gy2 = held([P, PACK, QUARTER], F32, "gy2_%d" % q)
+            for t in range(PACK):
+                nc.scalar.activation(
+                    gy2[:, t, :], gy[hf][t][:, side * QUARTER: (side + 1) * QUARTER], ACT.Square, bias=zero[:]
+                )
+            total[q] = held([P, PACK, QUARTER], F32, "total%d" % q)
+            nc.vector.tensor_tensor(total[q][:], gy2[:], gx2[hf][:, side], ADD)
+
+        def root(q):
+            h = held([P, PACK * QUARTER], BF16, "h%d" % q)
+            nc.scalar.activation(
+                h[:].rearrange("p (c i t) -> p c t i", i=4, t=PACK),
+                total[q][:].rearrange("p t (c i) -> p c t i", i=4),
+                ACT.Sqrt,
+            )
+            codes = held([P, QUARTER], U32, "h_codes%d" % q)
+            scales = held([P, QUARTER], U8, "h_scales%d" % q)
+            nc.vector.quantize_mx(out=codes[:].bitcast(FP8X4), scales=scales[:], in_=h[:])
+            hq[q] = codes, scales
+
+        def project(q):
+            codes, scales = hq[q]
+            for pair in range(2):
+                acc = psum.tile([P, 2, QUARTER], F32, name="bank%d" % (2 * q + pair))
+                for i in range(2):
+                    c = 2 * pair + i
+                    nc.tensor.matmul_mx(
+                        out=acc[:, i, :],
+                        lhsT=w4[:, 2 * P * c: 2 * P * (c + 1)].bitcast(FP4X4),
+                        lhsT_scale=w4_plane[:, P * c: P * (c + 1)],
+                        rhs=codes[:].bitcast(FP8X4),
+                        rhs_scale=scales[:],
+                        start=True,
+                        stop=True,
+                    )
+                res = held([P, 2, QUARTER], F32, "res%d_%d" % (q, pair))
+                for i in range(2):
+                    c = 2 * pair + i
+                    if q >= QUARTERS - 2 and pair == 1:
+                        nc.scalar.activation(res[:, i, :], acc[:, i, :], ACT.Identity, bias=bias_sb[:, c: c + 1])
+                    else:
+                        nc.vector.tensor_scalar_add(res[:, i, :], acc[:, i, :], bias_sb[:, c: c + 1])
+                nc.sync.dma_start(out_view[:, 2 * pair: 2 * pair + 2, q * QUARTER: (q + 1) * QUARTER], res[:])
+
+        square_add(0)
+        square_add(1)
+        root(0)
+        square_add(2)
+        root(1)
+        project(0)
+        square_add(3)
+        project(1)
+        root(2)
+        root(3)
+        project(2)
+        project(3)

@@ -24,6 +24,8 @@ HALF = 512
 HALVES = S // HALF
 QUARTER = 256
 QUARTERS = S // QUARTER
+SLOT = 8192
+PLACE = {"raw_x0": 0, "raw_x1": 1, "words1": 2, "raw_x2": 3, "raw_x3": 4, "raw_y0": 5, "raw_y1": 6, "raw_y2": 7, "raw_y3a": 8, "raw_y3b": 8.5, "bias_sb": 5, "words0": 10, "w4": 9}
 
 
 def tile_list_face_gradient_magnitudes_kernel(tc, tab, offs, wx, wy, w4_words, w4_scales, bias, out):
@@ -31,81 +33,77 @@ def tile_list_face_gradient_magnitudes_kernel(tc, tab, offs, wx, wy, w4_words, w
     with ExitStack() as ctx:
         keep = ctx.enter_context(tc.tile_pool(name="keep", bufs=1))
         ring = ctx.enter_context(tc.tile_pool(name="ring", bufs=4))
+        late = ctx.enter_context(tc.tile_pool(name="late", bufs=1))
         psum = ctx.enter_context(tc.psum_pool(name="psum", bufs=1))
 
-        def held(shape, dtype, name):
-            return keep.tile(shape, dtype, name=name, align_bytes=64)
+        def held(shape, dtype, name, tag=""):
+            return keep.tile(shape, dtype, name=name, tag=tag or name, align_bytes=64)
 
-        def streamed(shape, dtype, name):
-            return ring.tile(shape, dtype, name=name, tag="stream", align_bytes=64)
+        def placed(shape, dtype, name):
+            return late.tile(shape, dtype, name=name, offset=int(PLACE[name] * SLOT), align_bytes=64)
 
         offsets = keep.tile([P, S // 16], U16, name="offsets")
         nc.sync.dma_start(offsets[:], offs)
 
         tab_scales = held([P, T], U8, "tab_scales")
-        for quad in range(4):
-            nc.vector.memset(tab_scales[32 * quad: 32 * quad + 16, :].bitcast(I32), 0)
-        zero_in = held([P, 1], F32, "zero_in")
-        nc.vector.memset(zero_in[:], 0.0)
-        moved = [held([P, S], U8, "moved%d" % a) for a in range(PASSES)]
+        nc.vector.memset(tab_scales[:].bitcast(I32), 0)
+        zero_in = late.tile([P, 9 * SLOT // 4], F32, name="zero_in", offset=SLOT, align_bytes=64)
+        nc.vector.memset(zero_in[:, 0:1], 0.0)
+        moved = [held([P, S], U8, "moved%d" % a) for a in range(1, PASSES)]
         for plane in moved:
             nc.vector.memset(plane[:].bitcast(I32), 0)
-        w4_plane = held([P, N], U8, "w4_plane")
-        nc.gpsimd.memset(w4_plane[:], 0)
 
-        scale_rows = tab[:, 512 * T:].rearrange("m (h q t) -> m h q t", h=2, q=16)
-        for quad in range(4):
+        scale_rows = tab[:, 512 * T:].rearrange("m (h q r t) -> m r q h t", h=2, q=4, r=4)
+        for r in range(4):
             for m in range(2):
-                queue = nc.sync if quad == 0 else nc.scalar
-                queue.dma_start(
-                    tab_scales[32 * quad + 16 + 8 * m: 32 * quad + 24 + 8 * m, :].bitcast(I32),
-                    scale_rows[m, :, 4 * quad: 4 * quad + 4, :].bitcast(I32),
-                )
-        zero = held([P, 1], F32, "zero")
-        nc.scalar.activation(zero[:], zero_in[:], ACT.Sqrt)
+                queue = nc.gpsimd if r == 3 else nc.scalar
+                queue.dma_start(tab_scales[4 * m + r: P: 16, :].bitcast(I32), scale_rows[m, r].bitcast(I32))
+        zero = held([P, 1], F32, "zero", "grouped_last")
+        nc.scalar.activation(zero[:], zero_in[:, 0:1], ACT.Sqrt)
 
         def load_words(m):
-            words = streamed([P, T], I32, "words%d" % m)
+            words = placed([P, T], I32, "words%d" % m)
             nc.sync.dma_start(words[:], tab[m, : 512 * T].rearrange("(p b) -> p b", p=P).bitcast(I32))
             return words
 
         def load_weight(w, a, c0, c1, name):
-            raw = streamed([P, PACK, c1 - c0], F32, name)
+            raw = placed([P, PACK, c1 - c0], F32, name)
             rows = w[a * K_PASS: (a + 1) * K_PASS, c0:c1]
             nc.sync.dma_start(raw[:], rows.rearrange("(p j) c -> p j c", j=PACK))
             return raw
 
         raw_x, raw_y, words = [], [], []
         for a in range(PASSES):
-            if a == 2:
-                words.append(load_words(1))
+            if a % 2 == 0:
+                words.append(load_words(a // 2))
             raw_x.append(load_weight(wx, a, 0, H, "raw_x%d" % a))
-            if a == 0:
-                words.append(load_words(0))
         for a in range(PASSES - 1):
             raw_y.append(load_weight(wy, a, 0, H, "raw_y%d" % a))
         last_a = load_weight(wy, PASSES - 1, 0, H // 2, "raw_y3a")
         last_b = load_weight(wy, PASSES - 1, H // 2, H, "raw_y3b")
 
-        w4 = held([P, 2 * N], U8, "w4")
+        w4_plane = held([P, N], U8, "w4_plane")
+        nc.vector.memset(w4_plane[:].bitcast(I32), 0)
+        w4 = placed([P, 2 * N], U8, "w4")
         nc.gpsimd.dma_start(w4[:].bitcast(I32), w4_words[0].bitcast(I32))
         for quad in range(4):
             nc.gpsimd.dma_start(
                 w4_plane[32 * quad: 32 * quad + 4, :].bitcast(I32),
                 w4_scales[0, 4 * quad: 4 * quad + 4, :].bitcast(I32),
             )
-        bias_sb = streamed([P, N // P], F32, "bias_sb")
+        bias_sb = placed([P, N // P], F32, "bias_sb")
         with nc.allow_non_contiguous_dma(reason="one bias value for each partition and output tile"):
             nc.sync.dma_start(bias_sb[:], bias.rearrange("(c p) -> p c", p=P))
 
         picked_scales = held([P, S], U8, "picked_scales")
         nc.vector.tensor_copy(picked_scales[:], tab_scales[:].indirect(offsets[:]))
-        for a in range(PASSES):
-            nc.scalar.dma_start(
-                moved[a][0:100, :].bitcast(I32),
-                picked_scales[16 + 4 * a: 116 + 4 * a, :].bitcast(I32),
+        for a in range(1, PASSES):
+            shift = 16 * (a % 2) + 4 * (a // 2)
+            nc.gpsimd.dma_start(
+                moved[a - 1][0:100, :].bitcast(I32),
+                picked_scales[shift: shift + 100, :].bitcast(I32),
             )
-        planes = moved
+        planes = [picked_scales] + moved
 
         parted = {}
 
@@ -158,12 +156,15 @@ def tile_list_face_gradient_magnitudes_kernel(tc, tab, offs, wx, wy, w4_words, w
         gx = [banks(hf) for hf in range(HALVES)]
         for a in range(PASSES):
             grouped = new_grouped()
-            cast(nc.scalar.copy if a < PASSES - 1 else nc.vector.tensor_copy, grouped, raw_x[a], 0, P, 0)
+            if a < PASSES - 1:
+                cast(nc.scalar.copy, grouped, raw_x[a], 0, P, 0)
+            else:
+                cast(nc.scalar.copy, grouped, raw_x[a], 0, 64, 0)
+                cast(nc.vector.tensor_copy, grouped, raw_x[a], 64, P, 0)
             if a % 2 == 0:
                 gather(a // 2, 0)
-            weight = quantise(grouped, "wx%d" % a, 1)
-            if a % 2 == 0:
                 gather(a // 2, 1)
+            weight = quantise(grouped, "wx%d" % a, 1)
             for hf in range(HALVES):
                 multiply(gx[hf], weight, a, hf)
 
@@ -178,20 +179,22 @@ def tile_list_face_gradient_magnitudes_kernel(tc, tab, offs, wx, wy, w4_words, w
 
         wy_q = []
         for a in range(PASSES):
-            grouped = new_grouped()
             if a < PASSES - 1:
-                cast(nc.vector.tensor_copy, grouped, raw_y[a], 0, P, 0)
+                grouped = new_grouped()
+                if a == 0:
+                    cast(nc.scalar.copy, grouped, raw_y[a], 0, 64, 0)
+                    cast(nc.vector.tensor_copy, grouped, raw_y[a], 64, P, 0)
+                else:
+                    cast(nc.vector.tensor_copy, grouped, raw_y[a], 0, P, 0)
                 wy_q.append(quantise(grouped, "wy%d" % a, 1))
             else:
-                cast(nc.vector.tensor_copy, grouped, last_a, 0, 64, 0)
-                cast(nc.scalar.copy, grouped, last_b, 64, 84, 64)
-                cast(nc.vector.tensor_copy, grouped, last_b, 84, P, 64)
+                grouped = held([P, PACK * H], BF16, "grouped_last")
+                cast(nc.scalar.copy, grouped, last_a, 0, 64, 0)
+                cast(nc.vector.tensor_copy, grouped, last_b, 64, P, 64)
                 wy_q.append(quantise(grouped, "wy%d" % a, PACK))
-        gy = []
-        for hf in range(HALVES):
-            gy.append(banks(hf))
-            for a in range(PASSES):
-                multiply(gy[hf], wy_q[a], a, hf)
+        gy = [banks(hf) for hf in range(HALVES)]
+        for a, hf in ((0, 0), (0, 1), (1, 0), (1, 1), (2, 0), (3, 0), (2, 1), (3, 1)):
+            multiply(gy[hf], wy_q[a], a, hf)
 
         out_view = out.rearrange("(c p) j -> p c j", p=P)
         total = {}
@@ -202,7 +205,7 @@ def tile_list_face_gradient_magnitudes_kernel(tc, tab, offs, wx, wy, w4_words, w
             gy2 = held([P, PACK, QUARTER], F32, "gy2_%d" % q)
             for t in range(PACK):
                 nc.scalar.activation(
-                    gy2[:, t, :], gy[hf][t][:, side * QUARTER: (side + 1) * QUARTER], ACT.Square, bias=zero[:]
+                    gy2[:, t, :], gy[hf][t][:, side * QUARTER: (side + 1) * QUARTER], ACT.Square
                 )
             total[q] = held([P, PACK, QUARTER], F32, "total%d" % q)
             nc.vector.tensor_tensor(total[q][:], gy2[:], gx2[hf][:, side], ADD)

@@ -14,7 +14,6 @@ U8 = mybir.dt.uint8
 FP8X4 = mybir.dt.float8_e4m3fn_x4
 FP4X4 = mybir.dt.float4_e2m1fn_x4
 ACT = mybir.ActivationFunctionType
-ADD = mybir.AluOpType.add
 
 P = 128
 PACK = 4
@@ -22,239 +21,258 @@ K_PASS = P * PACK
 PASSES = K // K_PASS
 HALF = 512
 HALVES = S // HALF
-QUARTER = 256
-QUARTERS = S // QUARTER
+LIST_ROWS = 16
+
+RUNS = ((0, 256), (256, 256), (512, 256), (768, 128), (896, 128))
+
+SCALAR_SHARE_X = (128, 128, 76, 64)
+
+MOVED_ROWS = 108
+
 SLOT = 8192
-PLACE = {"raw_x0": 0, "raw_x1": 1, "words1": 2, "raw_x2": 3, "raw_x3": 4, "raw_y0": 5, "raw_y1": 6, "raw_y2": 7, "raw_y3a": 8, "raw_y3b": 8.5, "bias_sb": 5, "words0": 10, "w4": 9}
+PLACE = {
+    "words0": 0,
+    "raw_x0": SLOT,
+    "gate": 2 * SLOT,
+    "raw_x1": 2 * SLOT,
+    "words1": 3 * SLOT,
+    "raw_x2": 4 * SLOT,
+    "rounded_x0": 5 * SLOT,
+    "raw_x3": 5 * SLOT,
+    "raw_y0": 2 * SLOT,
+    "raw_y1": 3 * SLOT,
+    "raw_y2": 4 * SLOT,
+    "raw_y3_low": 5 * SLOT,
+    "raw_y3_high": 5 * SLOT + SLOT // 2,
+    "w4": 2 * SLOT,
+    "w4_scale": 2 * SLOT + SLOT // 4,
+    "bias_sb": 2 * SLOT + SLOT // 2,
+}
 
 
 def tile_list_face_gradient_magnitudes_kernel(tc, tab, offs, wx, wy, w4_words, w4_scales, bias, out):
     nc = tc.nc
     with ExitStack() as ctx:
         keep = ctx.enter_context(tc.tile_pool(name="keep", bufs=1))
-        ring = ctx.enter_context(tc.tile_pool(name="ring", bufs=4))
-        late = ctx.enter_context(tc.tile_pool(name="late", bufs=1))
+        loaded = ctx.enter_context(tc.tile_pool(name="loaded", bufs=1))
+        ring = ctx.enter_context(tc.tile_pool(name="ring", bufs=PASSES))
         psum = ctx.enter_context(tc.psum_pool(name="psum", bufs=1))
 
-        def held(shape, dtype, name, tag=""):
+        def held(shape, dtype, name, tag=None):
             return keep.tile(shape, dtype, name=name, tag=tag or name, align_bytes=64)
 
         def placed(shape, dtype, name):
-            return late.tile(shape, dtype, name=name, offset=int(PLACE[name] * SLOT), align_bytes=64)
+            return loaded.tile(shape, dtype, name=name, offset=PLACE[name], align_bytes=64)
 
-        offsets = keep.tile([P, S // 16], U16, name="offsets")
+        offsets = keep.tile([P, S // LIST_ROWS], U16, name="offsets")
         nc.sync.dma_start(offsets[:], offs)
 
-        tab_scales = held([P, T], U8, "tab_scales")
-        nc.vector.memset(tab_scales[:].bitcast(I32), 0)
-        zero_in = late.tile([P, 9 * SLOT // 4], F32, name="zero_in", offset=SLOT, align_bytes=64)
-        nc.vector.memset(zero_in[:, 0:1], 0.0)
-        moved = [held([P, S], U8, "moved%d" % a) for a in range(1, PASSES)]
-        for plane in moved:
-            nc.vector.memset(plane[:].bitcast(I32), 0)
+        tab_scale = held([P, T], U8, "tab_scale")
+        nc.vector.memset(tab_scale[:].bitcast(I32), 0)
+        gate = placed([P, 3 * SLOT // 4], F32, "gate")
+        nc.vector.memset(gate[:, 0:1], 0.0)
+        moved_scale = [held([P, S], U8, "moved_scale%d" % a) for a in range(1, PASSES)]
+        for tile in moved_scale:
+            nc.vector.memset(tile[:].bitcast(I32), 0)
 
-        scale_rows = tab[:, 512 * T:].rearrange("m (h q r t) -> m r q h t", h=2, q=4, r=4)
+        scale_rows = tab[:, K_PASS * T:].rearrange("m (h q r t) -> m r q h t", h=2, q=4, r=4)
         for r in range(4):
             for m in range(2):
                 queue = nc.gpsimd if r == 3 else nc.scalar
-                queue.dma_start(tab_scales[4 * m + r: P: 16, :].bitcast(I32), scale_rows[m, r].bitcast(I32))
-        zero = held([P, 1], F32, "zero", "grouped_last")
-        nc.scalar.activation(zero[:], zero_in[:, 0:1], ACT.Sqrt)
+                queue.dma_start(tab_scale[4 * m + r: P: 16, :].bitcast(I32), scale_rows[m, r].bitcast(I32))
+
+        zero = held([P, 1], F32, "zero", "rounded_last")
+        nc.scalar.activation(zero[:], gate[:, 0:1], ACT.Sqrt)
 
         def load_words(m):
-            words = placed([P, T], I32, "words%d" % m)
-            nc.sync.dma_start(words[:], tab[m, : 512 * T].rearrange("(p b) -> p b", p=P).bitcast(I32))
-            return words
+            tile = placed([P, T], I32, "words%d" % m)
+            nc.sync.dma_start(tile[:], tab[m, : K_PASS * T].rearrange("(p b) -> p b", p=P).bitcast(I32))
+            return tile
 
-        def load_weight(w, a, c0, c1, name):
-            raw = placed([P, PACK, c1 - c0], F32, name)
-            rows = w[a * K_PASS: (a + 1) * K_PASS, c0:c1]
-            nc.sync.dma_start(raw[:], rows.rearrange("(p j) c -> p j c", j=PACK))
-            return raw
+        def load_weight(w, a, cols, name):
+            rows = w[a * K_PASS: (a + 1) * K_PASS, cols]
+            tile = placed([P, PACK, rows.shape[1]], F32, name)
+            nc.sync.dma_start(tile[:], rows.rearrange("(p i) c -> p i c", i=PACK))
+            return tile
 
-        raw_x, raw_y, words = [], [], []
-        for a in range(PASSES):
-            if a % 2 == 0:
-                words.append(load_words(a // 2))
-            raw_x.append(load_weight(wx, a, 0, H, "raw_x%d" % a))
-        for a in range(PASSES - 1):
-            raw_y.append(load_weight(wy, a, 0, H, "raw_y%d" % a))
-        last_a = load_weight(wy, PASSES - 1, 0, H // 2, "raw_y3a")
-        last_b = load_weight(wy, PASSES - 1, H // 2, H, "raw_y3b")
-
-        w4_plane = held([P, N], U8, "w4_plane")
-        nc.vector.memset(w4_plane[:].bitcast(I32), 0)
-        w4 = placed([P, 2 * N], U8, "w4")
-        nc.gpsimd.dma_start(w4[:].bitcast(I32), w4_words[0].bitcast(I32))
-        for quad in range(4):
-            nc.gpsimd.dma_start(
-                w4_plane[32 * quad: 32 * quad + 4, :].bitcast(I32),
-                w4_scales[0, 4 * quad: 4 * quad + 4, :].bitcast(I32),
-            )
-        bias_sb = placed([P, N // P], F32, "bias_sb")
-        with nc.allow_non_contiguous_dma(reason="one bias value for each partition and output tile"):
-            nc.sync.dma_start(bias_sb[:], bias.rearrange("(c p) -> p c", p=P))
-
-        picked_scales = held([P, S], U8, "picked_scales")
-        nc.vector.tensor_copy(picked_scales[:], tab_scales[:].indirect(offsets[:]))
-        for a in range(1, PASSES):
+        def move_scale(a):
             shift = 16 * (a % 2) + 4 * (a // 2)
-            nc.gpsimd.dma_start(
-                moved[a - 1][0:100, :].bitcast(I32),
-                picked_scales[shift: shift + 100, :].bitcast(I32),
+            nc.sync.dma_start(
+                moved_scale[a - 1][0:MOVED_ROWS, :].bitcast(I32),
+                picked_scale[shift: shift + MOVED_ROWS, :].bitcast(I32),
             )
-        planes = [picked_scales] + moved
 
-        parted = {}
-
-        def gather(m, hf):
+        def gather_words(m, hf):
             picked = held([P, HALF], U32, "picked%d_%d" % (m, hf))
-            cols = slice(hf * HALF // 16, (hf + 1) * HALF // 16)
-            nc.vector.tensor_copy(picked[:], words[m][:].bitcast(U32).indirect(offsets[:, cols]))
-            part = held([P, 2, HALF], U16, "parted%d_%d" % (m, hf))
-            nc.vector.tensor_copy(part[:], picked[:].bitcast(U16).rearrange("p (s h) -> p h s", h=2))
-            parted[m, hf] = part
+            entries = offsets[:, hf * HALF // LIST_ROWS: (hf + 1) * HALF // LIST_ROWS]
+            nc.vector.tensor_copy(picked[:], words[m][:].bitcast(U32).indirect(entries))
+            parted = held([P, 2, HALF], U16, "parted%d_%d" % (m, hf))
+            nc.vector.tensor_copy(parted[:], picked[:].bitcast(U16).rearrange("p (s h) -> p h s", h=2))
+            table[2 * m, hf] = parted[:, 0, :]
+            table[2 * m + 1, hf] = parted[:, 1, :]
 
-        def cast(engine_copy, grouped, raw, m0, m1, base):
-            dst = grouped[:].rearrange("p (t m j) -> p m j t", t=PACK, j=PACK)[:, m0:m1]
-            src = raw[:].rearrange("p j (m t) -> p m j t", t=PACK)[:, m0 - base: m1 - base]
-            engine_copy(dst, src)
+        def round_weight(copy, rounded, raw, first, last, base=0):
+            copy(
+                rounded[:].rearrange("p (t m i) -> p m i t", t=PACK, i=PACK)[:, first:last],
+                raw[:].rearrange("p i (m t) -> p m i t", t=PACK)[:, first - base: last - base],
+            )
 
-        def new_grouped():
-            return ring.tile([P, PACK * H], BF16, name="grouped", align_bytes=64)
+        def round_shared(rounded, raw, share):
+            if share > 0:
+                round_weight(nc.scalar.copy, rounded, raw, 0, share)
+            if share < P:
+                round_weight(nc.vector.tensor_copy, rounded, raw, share, P)
 
-        def quantise(grouped, name, pieces):
-            codes = held([P, H], U32, name + "_codes")
-            scales = held([P, H], U8, name + "_scales")
-            width = H // pieces
-            for i in range(pieces):
-                cols = slice(i * width, (i + 1) * width)
+        def quantise(rounded, name, pieces=1):
+            columns = rounded.shape[1] // PACK
+            codes = held([P, columns], U32, name + "_codes")
+            scale = held([P, columns], U8, name + "_scale")
+            width = columns // pieces
+            for c0 in range(0, columns, width):
                 nc.vector.quantize_mx(
-                    out=codes[:, cols].bitcast(FP8X4),
-                    scales=scales[:, cols],
-                    in_=grouped[:, PACK * i * width: PACK * (i + 1) * width],
+                    out=codes[:, c0: c0 + width].bitcast(FP8X4),
+                    scales=scale[:, c0: c0 + width],
+                    in_=rounded[:, PACK * c0: PACK * (c0 + width)],
                 )
-            return codes, scales
+            return codes, scale
 
         def banks(hf):
-            return [psum.tile([P, HALF], F32, name="bank%d" % (4 * hf + t)) for t in range(PACK)]
+            return [psum.tile([P, HALF], F32, name="bank%d" % (PACK * hf + t)) for t in range(PACK)]
 
-        def multiply(acc, weight, a, hf):
-            codes, scales = weight
+        def multiply(acc, weight, a, hf, start, stop):
+            codes, scale = weight
             for t in range(PACK):
                 cols = slice(t * P, (t + 1) * P)
                 nc.tensor.matmul_mx(
                     out=acc[t][:],
                     lhsT=codes[:, cols].bitcast(FP8X4),
-                    lhsT_scale=scales[:, cols],
-                    rhs=parted[a // 2, hf][:, a % 2, :].bitcast(FP4X4),
-                    rhs_scale=planes[a][:, hf * HALF: (hf + 1) * HALF],
-                    start=(a == 0),
-                    stop=(a == PASSES - 1),
+                    lhsT_scale=scale[:, cols],
+                    rhs=table[a, hf].bitcast(FP4X4),
+                    rhs_scale=table_scale[a][:, hf * HALF: (hf + 1) * HALF],
+                    start=start,
+                    stop=stop,
                 )
+
+        whole = slice(0, H)
+        words = [load_words(0)]
+        raw_x = [load_weight(wx, 0, whole, "raw_x0"), load_weight(wx, 1, whole, "raw_x1")]
+        words.append(load_words(1))
+        raw_x.append(load_weight(wx, 2, whole, "raw_x2"))
+
+        picked_scale = held([P, S], U8, "picked_scale")
+        nc.vector.tensor_copy(picked_scale[:], tab_scale[:].indirect(offsets[:]))
+        table_scale = [picked_scale] + moved_scale
+        table = {}
+
+        rounded = placed([P, PACK * H], BF16, "rounded_x0")
+        round_shared(rounded, raw_x[0], SCALAR_SHARE_X[0])
+        for hf in range(HALVES):
+            gather_words(0, hf)
+        wx_mx = [quantise(rounded, "wx0")]
+
+        move_scale(1)
+        raw_x.append(load_weight(wx, 3, whole, "raw_x3"))
+        move_scale(2)
+        move_scale(3)
+        raw_y = [load_weight(wy, a, whole, "raw_y%d" % a) for a in range(PASSES - 1)]
+        raw_y_low = load_weight(wy, PASSES - 1, slice(0, H // 2), "raw_y3_low")
+        raw_y_high = load_weight(wy, PASSES - 1, slice(H // 2, H), "raw_y3_high")
+
+        w4 = placed([P, 2 * N], U8, "w4")
+        nc.sync.dma_start(w4[:].bitcast(I32), w4_words[0].bitcast(I32))
+        w4_scale = placed([P, N], U8, "w4_scale")
+        nc.vector.memset(w4_scale[:].bitcast(I32), 0)
+        for q in range(4):
+            nc.sync.dma_start(
+                w4_scale[32 * q: 32 * q + 4, :].bitcast(I32), w4_scales[0, 4 * q: 4 * q + 4, :].bitcast(I32)
+            )
+        bias_sb = placed([P, N // P], F32, "bias_sb")
+        with nc.allow_non_contiguous_dma(reason="one bias value for each partition and output tile"):
+            nc.sync.dma_start(bias_sb[:], bias.rearrange("(c p) -> p c", p=P))
 
         gx = [banks(hf) for hf in range(HALVES)]
         for a in range(PASSES):
-            grouped = new_grouped()
-            if a < PASSES - 1:
-                cast(nc.scalar.copy, grouped, raw_x[a], 0, P, 0)
-            else:
-                cast(nc.scalar.copy, grouped, raw_x[a], 0, 64, 0)
-                cast(nc.vector.tensor_copy, grouped, raw_x[a], 64, P, 0)
-            if a % 2 == 0:
-                gather(a // 2, 0)
-                gather(a // 2, 1)
-            weight = quantise(grouped, "wx%d" % a, 1)
+            if a > 0:
+                rounded = ring.tile([P, PACK * H], BF16, name="rounded", align_bytes=64)
+                round_shared(rounded, raw_x[a], SCALAR_SHARE_X[a])
+                if a % 2 == 0:
+                    for hf in range(HALVES):
+                        gather_words(a // 2, hf)
+                wx_mx.append(quantise(rounded, "wx%d" % a))
             for hf in range(HALVES):
-                multiply(gx[hf], weight, a, hf)
+                multiply(gx[hf], wx_mx[a], a, hf, start=(a == 0), stop=(a == PASSES - 1))
 
-        gx2 = []
+        gx2 = [held([P, PACK, HALF], F32, "gx2_%d" % hf) for hf in range(HALVES)]
         for hf in range(HALVES):
-            sq = held([P, 2, PACK, QUARTER], F32, "gx2_%d" % hf)
             for t in range(PACK):
-                nc.scalar.activation(
-                    sq[:, :, t, :], gx[hf][t][:].rearrange("p (q j) -> p q j", q=2), ACT.Square, bias=zero[:]
-                )
-            gx2.append(sq)
+                nc.scalar.activation(gx2[hf][:, t, :], gx[hf][t][:], ACT.Square, bias=zero[:])
 
-        wy_q = []
-        for a in range(PASSES):
-            if a < PASSES - 1:
-                grouped = new_grouped()
-                if a == 0:
-                    cast(nc.scalar.copy, grouped, raw_y[a], 0, 64, 0)
-                    cast(nc.vector.tensor_copy, grouped, raw_y[a], 64, P, 0)
-                else:
-                    cast(nc.vector.tensor_copy, grouped, raw_y[a], 0, P, 0)
-                wy_q.append(quantise(grouped, "wy%d" % a, 1))
-            else:
-                grouped = held([P, PACK * H], BF16, "grouped_last")
-                cast(nc.scalar.copy, grouped, last_a, 0, 64, 0)
-                cast(nc.vector.tensor_copy, grouped, last_b, 64, P, 64)
-                wy_q.append(quantise(grouped, "wy%d" % a, PACK))
+        wy_mx = []
+        for a in range(PASSES - 1):
+            rounded = ring.tile([P, PACK * H], BF16, name="rounded", align_bytes=64)
+            round_weight(nc.vector.tensor_copy, rounded, raw_y[a], 0, P)
+            wy_mx.append(quantise(rounded, "wy%d" % a))
+        rounded = held([P, PACK * H], BF16, "rounded_last")
+        round_weight(nc.scalar.copy, rounded, raw_y_low, 0, P // 2)
+        round_weight(nc.vector.tensor_copy, rounded, raw_y_high, P // 2, P, base=P // 2)
+        wy_mx.append(quantise(rounded, "wy3", pieces=PACK))
+
         gy = [banks(hf) for hf in range(HALVES)]
-        for a, hf in ((0, 0), (0, 1), (1, 0), (1, 1), (2, 0), (3, 0), (2, 1), (3, 1)):
-            multiply(gy[hf], wy_q[a], a, hf)
+        for hf, order in enumerate(((0, 1, 2, 3), (0, 3, 1, 2))):
+            for a in order:
+                multiply(gy[hf], wy_mx[a], a, hf, start=(a == order[0]), stop=(a == order[-1]))
 
-        out_view = out.rearrange("(c p) j -> p c j", p=P)
-        total = {}
-        hq = {}
+        out_tiles = out.rearrange("(c p) j -> p c j", p=P)
+        sums, h_mx = {}, {}
 
-        def square_add(q):
-            hf, side = divmod(q, 2)
-            gy2 = held([P, PACK, QUARTER], F32, "gy2_%d" % q)
+        def square_and_add(run):
+            first, count = RUNS[run]
+            hf = first // HALF
+            cols = slice(first % HALF, first % HALF + count)
+            gy2 = held([P, PACK, count], F32, "gy2_%d" % run)
             for t in range(PACK):
-                nc.scalar.activation(
-                    gy2[:, t, :], gy[hf][t][:, side * QUARTER: (side + 1) * QUARTER], ACT.Square
-                )
-            total[q] = held([P, PACK, QUARTER], F32, "total%d" % q)
-            nc.vector.tensor_tensor(total[q][:], gy2[:], gx2[hf][:, side], ADD)
+                nc.scalar.activation(gy2[:, t, :], gy[hf][t][:, cols], ACT.Square)
+            sums[run] = held([P, PACK, count], F32, "sum%d" % run)
+            nc.vector.tensor_add(sums[run][:], gy2[:], gx2[hf][:, :, cols])
 
-        def root(q):
-            h = held([P, PACK * QUARTER], BF16, "h%d" % q)
+        def root(run):
+            h = held([P, PACK * RUNS[run][1]], BF16, "h%d" % run)
             nc.scalar.activation(
                 h[:].rearrange("p (c i t) -> p c t i", i=4, t=PACK),
-                total[q][:].rearrange("p t (c i) -> p c t i", i=4),
+                sums[run][:].rearrange("p t (c i) -> p c t i", i=4),
                 ACT.Sqrt,
             )
-            codes = held([P, QUARTER], U32, "h_codes%d" % q)
-            scales = held([P, QUARTER], U8, "h_scales%d" % q)
-            nc.vector.quantize_mx(out=codes[:].bitcast(FP8X4), scales=scales[:], in_=h[:])
-            hq[q] = codes, scales
+            h_mx[run] = quantise(h, "h%d" % run)
 
-        def project(q):
-            codes, scales = hq[q]
+        def project(run):
+            first, count = RUNS[run]
+            codes, scale = h_mx[run]
             for pair in range(2):
-                acc = psum.tile([P, 2, QUARTER], F32, name="bank%d" % (2 * q + pair))
+                acc = psum.tile([P, 2, count], F32, name="bank%d" % ((2 * run + pair) % PACK))
                 for i in range(2):
                     c = 2 * pair + i
                     nc.tensor.matmul_mx(
                         out=acc[:, i, :],
                         lhsT=w4[:, 2 * P * c: 2 * P * (c + 1)].bitcast(FP4X4),
-                        lhsT_scale=w4_plane[:, P * c: P * (c + 1)],
+                        lhsT_scale=w4_scale[:, P * c: P * (c + 1)],
                         rhs=codes[:].bitcast(FP8X4),
-                        rhs_scale=scales[:],
+                        rhs_scale=scale[:],
                         start=True,
                         stop=True,
                     )
-                res = held([P, 2, QUARTER], F32, "res%d_%d" % (q, pair))
+                res = held([P, 2, count], F32, "res%d_%d" % (run, pair))
                 for i in range(2):
-                    c = 2 * pair + i
-                    if q >= QUARTERS - 2 and pair == 1:
-                        nc.scalar.activation(res[:, i, :], acc[:, i, :], ACT.Identity, bias=bias_sb[:, c: c + 1])
+                    column = bias_sb[:, 2 * pair + i: 2 * pair + i + 1]
+                    if run >= len(RUNS) - 2 and pair == 1:
+                        nc.scalar.activation(res[:, i, :], acc[:, i, :], ACT.Identity, bias=column)
                     else:
-                        nc.vector.tensor_scalar_add(res[:, i, :], acc[:, i, :], bias_sb[:, c: c + 1])
-                nc.sync.dma_start(out_view[:, 2 * pair: 2 * pair + 2, q * QUARTER: (q + 1) * QUARTER], res[:])
+                        nc.vector.tensor_scalar_add(res[:, i, :], acc[:, i, :], column)
+                nc.sync.dma_start(out_tiles[:, 2 * pair: 2 * pair + 2, first: first + count], res[:])
 
-        square_add(0)
-        square_add(1)
-        root(0)
-        square_add(2)
-        root(1)
-        project(0)
-        square_add(3)
-        project(1)
-        root(2)
-        root(3)
-        project(2)
-        project(3)
+        for step in range(len(RUNS) + 2):
+            if step < len(RUNS):
+                square_and_add(step)
+            if 1 <= step <= len(RUNS):
+                root(step - 1)
+            if step >= 2:
+                project(step - 2)

@@ -25,7 +25,7 @@ LIST_ROWS = 16
 
 RUNS = ((0, 256), (256, 256), (512, 256), (768, 128), (896, 128))
 
-SCALAR_SHARE_X = (128, 128, 76, 64)
+SCALAR_PAIRS_X = (2, 2, 1, 1)
 
 MOVED_ROWS = 108
 
@@ -111,17 +111,16 @@ def tile_list_face_gradient_magnitudes_kernel(tc, tab, offs, wx, wy, w4_words, w
             table[2 * m, hf] = parted[:, 0, :]
             table[2 * m + 1, hf] = parted[:, 1, :]
 
-        def round_weight(copy, rounded, raw, first, last, base=0):
-            copy(
-                rounded[:].rearrange("p (t m i) -> p m i t", t=PACK, i=PACK)[:, first:last],
-                raw[:].rearrange("p i (m t) -> p m i t", t=PACK)[:, first - base: last - base],
-            )
+        def round_weight(copy, rounded, raw, pairs, base=0):
+            groups = raw.shape[2] // (2 * PACK)
+            dst = rounded[:].rearrange("p (u e g f i) -> p u g i f e", u=2, e=2, f=2, i=PACK)
+            src = raw[:].rearrange("p i (g f u e) -> p u g i f e", f=2, u=2, e=2)
+            for u in pairs:
+                copy(dst[:, u, base // 2: base // 2 + groups], src[:, u])
 
-        def round_shared(rounded, raw, share):
-            if share > 0:
-                round_weight(nc.scalar.copy, rounded, raw, 0, share)
-            if share < P:
-                round_weight(nc.vector.tensor_copy, rounded, raw, share, P)
+        def round_x(rounded, a):
+            round_weight(nc.scalar.copy, rounded, raw_x[a], range(SCALAR_PAIRS_X[a]))
+            round_weight(nc.vector.tensor_copy, rounded, raw_x[a], range(SCALAR_PAIRS_X[a], 2))
 
         def quantise(rounded, name, pieces=1):
             columns = rounded.shape[1] // PACK
@@ -165,7 +164,7 @@ def tile_list_face_gradient_magnitudes_kernel(tc, tab, offs, wx, wy, w4_words, w
         table = {}
 
         rounded = placed([P, PACK * H], BF16, "rounded_x0")
-        round_shared(rounded, raw_x[0], SCALAR_SHARE_X[0])
+        round_x(rounded, 0)
         for hf in range(HALVES):
             gather_words(0, hf)
         wx_mx = [quantise(rounded, "wx0")]
@@ -194,7 +193,7 @@ def tile_list_face_gradient_magnitudes_kernel(tc, tab, offs, wx, wy, w4_words, w
         for a in range(PASSES):
             if a > 0:
                 rounded = ring.tile([P, PACK * H], BF16, name="rounded", align_bytes=64)
-                round_shared(rounded, raw_x[a], SCALAR_SHARE_X[a])
+                round_x(rounded, a)
                 if a % 2 == 0:
                     for hf in range(HALVES):
                         gather_words(a // 2, hf)
@@ -210,11 +209,11 @@ def tile_list_face_gradient_magnitudes_kernel(tc, tab, offs, wx, wy, w4_words, w
         wy_mx = []
         for a in range(PASSES - 1):
             rounded = ring.tile([P, PACK * H], BF16, name="rounded", align_bytes=64)
-            round_weight(nc.vector.tensor_copy, rounded, raw_y[a], 0, P)
+            round_weight(nc.vector.tensor_copy, rounded, raw_y[a], range(2))
             wy_mx.append(quantise(rounded, "wy%d" % a))
         rounded = held([P, PACK * H], BF16, "rounded_last")
-        round_weight(nc.scalar.copy, rounded, raw_y_low, 0, P // 2)
-        round_weight(nc.vector.tensor_copy, rounded, raw_y_high, P // 2, P, base=P // 2)
+        round_weight(nc.scalar.copy, rounded, raw_y_low, range(2))
+        round_weight(nc.vector.tensor_copy, rounded, raw_y_high, range(2), base=P // 2)
         wy_mx.append(quantise(rounded, "wy3", pieces=PACK))
 
         gy = [banks(hf) for hf in range(HALVES)]

@@ -25,6 +25,8 @@ LIST_ROWS = 16
 
 RUNS = ((0, 256), (256, 256), (512, 256), (768, 128), (896, 128))
 
+SHARED_RUNS = 2
+
 SCALAR_PAIRS_X = (2, 2, 1, 1)
 
 MOVED_ROWS = 108
@@ -75,41 +77,44 @@ def tile_list_face_gradient_magnitudes_kernel(tc, tab, offs, wx, wy, w4_words, w
         for tile in moved_scale:
             nc.vector.memset(tile[:].bitcast(I32), 0)
 
-        scale_rows = tab[:, K_PASS * T:].rearrange("m (h q r t) -> m r q h t", h=2, q=4, r=4)
-        for r in range(4):
-            for m in range(2):
-                queue = nc.gpsimd if r == 3 else nc.scalar
-                queue.dma_start(tab_scale[4 * m + r: P: 16, :].bitcast(I32), scale_rows[m, r].bitcast(I32))
+        scale_rows = tab[:, K_PASS * T:].rearrange("d (w Q b vertex) -> d b Q w vertex", w=2, Q=4, b=4)
+        for b in range(4):
+            for d in range(2):
+                queue = nc.gpsimd if b == 3 else nc.scalar
+                queue.dma_start(tab_scale[4 * d + b: P: 16, :].bitcast(I32), scale_rows[d, b].bitcast(I32))
 
         zero = held([P, 1], F32, "zero", "rounded_last")
         nc.scalar.activation(zero[:], gate[:, 0:1], ACT.Sqrt)
 
-        def load_words(m):
-            tile = placed([P, T], I32, "words%d" % m)
-            nc.sync.dma_start(tile[:], tab[m, : K_PASS * T].rearrange("(p b) -> p b", p=P).bitcast(I32))
+        def load_words(d):
+            tile = placed([P, T], I32, "words%d" % d)
+            nc.sync.dma_start(tile[:], tab[d, : K_PASS * T].rearrange("(p x) -> p x", p=P).bitcast(I32))
             return tile
 
-        def load_weight(w, a, cols, name):
-            rows = w[a * K_PASS: (a + 1) * K_PASS, cols]
+        def load_weight(weight, a, cols, name):
+            rows = weight[a * K_PASS: (a + 1) * K_PASS, cols]
             tile = placed([P, PACK, rows.shape[1]], F32, name)
-            nc.sync.dma_start(tile[:], rows.rearrange("(p i) c -> p i c", i=PACK))
+            nc.sync.dma_start(tile[:], rows.rearrange("(p i) x -> p i x", i=PACK))
             return tile
 
         def move_scale(a):
-            shift = 16 * (a % 2) + 4 * (a // 2)
+            d, w = divmod(a, 2)
+            shift = 16 * w + 4 * d
             nc.sync.dma_start(
                 moved_scale[a - 1][0:MOVED_ROWS, :].bitcast(I32),
                 picked_scale[shift: shift + MOVED_ROWS, :].bitcast(I32),
             )
 
-        def gather_words(m, hf):
-            picked = held([P, HALF], U32, "picked%d_%d" % (m, hf))
-            entries = offsets[:, hf * HALF // LIST_ROWS: (hf + 1) * HALF // LIST_ROWS]
-            nc.vector.tensor_copy(picked[:], words[m][:].bitcast(U32).indirect(entries))
-            parted = held([P, 2, HALF], U16, "parted%d_%d" % (m, hf))
-            nc.vector.tensor_copy(parted[:], picked[:].bitcast(U16).rearrange("p (s h) -> p h s", h=2))
-            table[2 * m, hf] = parted[:, 0, :]
-            table[2 * m + 1, hf] = parted[:, 1, :]
+        def gather_words(d):
+            picked = [held([P, HALF], U32, "picked%d_%d" % (d, hf)) for hf in range(HALVES)]
+            for hf in range(HALVES):
+                entries = offsets[:, hf * HALF // LIST_ROWS: (hf + 1) * HALF // LIST_ROWS]
+                nc.vector.tensor_copy(picked[hf][:], words[d][:].bitcast(U32).indirect(entries))
+            for hf in range(HALVES):
+                parted = held([P, 2, HALF], U16, "parted%d_%d" % (d, hf))
+                nc.vector.tensor_copy(parted[:], picked[hf][:].bitcast(U16).rearrange("p (j w) -> p w j", w=2))
+                for w in range(2):
+                    table[2 * d + w, hf] = parted[:, w, :]
 
         def round_weight(copy, rounded, raw, pairs, base=0):
             groups = raw.shape[2] // (2 * PACK)
@@ -138,9 +143,9 @@ def tile_list_face_gradient_magnitudes_kernel(tc, tab, offs, wx, wy, w4_words, w
         def banks(hf):
             return [psum.tile([P, HALF], F32, name="bank%d" % (PACK * hf + t)) for t in range(PACK)]
 
-        def multiply(acc, weight, a, hf, start, stop):
-            codes, scale = weight
-            for t in range(PACK):
+        def multiply(acc, weight_mx, a, hf, start, stop, tiles=range(PACK)):
+            codes, scale = weight_mx
+            for t in tiles:
                 cols = slice(t * P, (t + 1) * P)
                 nc.tensor.matmul_mx(
                     out=acc[t][:],
@@ -165,9 +170,8 @@ def tile_list_face_gradient_magnitudes_kernel(tc, tab, offs, wx, wy, w4_words, w
 
         rounded = placed([P, PACK * H], BF16, "rounded_x0")
         round_x(rounded, 0)
-        for hf in range(HALVES):
-            gather_words(0, hf)
-        wx_mx = [quantise(rounded, "wx0")]
+        gather_words(0)
+        wx_mx = [quantise(rounded, "wx0", pieces=2)]
 
         move_scale(1)
         raw_x.append(load_weight(wx, 3, whole, "raw_x3"))
@@ -181,9 +185,9 @@ def tile_list_face_gradient_magnitudes_kernel(tc, tab, offs, wx, wy, w4_words, w
         nc.sync.dma_start(w4[:].bitcast(I32), w4_words[0].bitcast(I32))
         w4_scale = placed([P, N], U8, "w4_scale")
         nc.vector.memset(w4_scale[:].bitcast(I32), 0)
-        for q in range(4):
+        for Q in range(4):
             nc.sync.dma_start(
-                w4_scale[32 * q: 32 * q + 4, :].bitcast(I32), w4_scales[0, 4 * q: 4 * q + 4, :].bitcast(I32)
+                w4_scale[32 * Q: 32 * Q + 4, :].bitcast(I32), w4_scales[0, 4 * Q: 4 * Q + 4, :].bitcast(I32)
             )
         bias_sb = placed([P, N // P], F32, "bias_sb")
         with nc.allow_non_contiguous_dma(reason="one bias value for each partition and output tile"):
@@ -195,9 +199,8 @@ def tile_list_face_gradient_magnitudes_kernel(tc, tab, offs, wx, wy, w4_words, w
                 rounded = ring.tile([P, PACK * H], BF16, name="rounded", align_bytes=64)
                 round_x(rounded, a)
                 if a % 2 == 0:
-                    for hf in range(HALVES):
-                        gather_words(a // 2, hf)
-                wx_mx.append(quantise(rounded, "wx%d" % a))
+                    gather_words(a // 2)
+                wx_mx.append(quantise(rounded, "wx%d" % a, pieces=2))
             for hf in range(HALVES):
                 multiply(gx[hf], wx_mx[a], a, hf, start=(a == 0), stop=(a == PASSES - 1))
 
@@ -210,16 +213,20 @@ def tile_list_face_gradient_magnitudes_kernel(tc, tab, offs, wx, wy, w4_words, w
         for a in range(PASSES - 1):
             rounded = ring.tile([P, PACK * H], BF16, name="rounded", align_bytes=64)
             round_weight(nc.vector.tensor_copy, rounded, raw_y[a], range(2))
-            wy_mx.append(quantise(rounded, "wy%d" % a))
+            wy_mx.append(quantise(rounded, "wy%d" % a, pieces=2))
         rounded = held([P, PACK * H], BF16, "rounded_last")
         round_weight(nc.scalar.copy, rounded, raw_y_low, range(2))
         round_weight(nc.vector.tensor_copy, rounded, raw_y_high, range(2), base=P // 2)
         wy_mx.append(quantise(rounded, "wy3", pieces=PACK))
 
         gy = [banks(hf) for hf in range(HALVES)]
-        for hf, order in enumerate(((0, 1, 2, 3), (0, 3, 1, 2))):
-            for a in order:
-                multiply(gy[hf], wy_mx[a], a, hf, start=(a == order[0]), stop=(a == order[-1]))
+        for a in range(PASSES):
+            multiply(gy[0], wy_mx[a], a, 0, start=(a == 0), stop=(a == PASSES - 1))
+        for a in (0, 3):
+            multiply(gy[1], wy_mx[a], a, 1, start=(a == 0), stop=False)
+        for t in range(PACK):
+            for a in (1, 2):
+                multiply(gy[1], wy_mx[a], a, 1, start=False, stop=(a == 2), tiles=(t,))
 
         out_tiles = out.rearrange("(c p) j -> p c j", p=P)
         sums, h_mx = {}, {}
@@ -237,8 +244,8 @@ def tile_list_face_gradient_magnitudes_kernel(tc, tab, offs, wx, wy, w4_words, w
         def root(run):
             h = held([P, PACK * RUNS[run][1]], BF16, "h%d" % run)
             nc.scalar.activation(
-                h[:].rearrange("p (c i t) -> p c t i", i=4, t=PACK),
-                sums[run][:].rearrange("p t (c i) -> p c t i", i=4),
+                h[:].rearrange("p (four j t) -> p four t j", j=4, t=PACK),
+                sums[run][:].rearrange("p t (four j) -> p four t j", j=4),
                 ACT.Sqrt,
             )
             h_mx[run] = quantise(h, "h%d" % run)
@@ -248,10 +255,10 @@ def tile_list_face_gradient_magnitudes_kernel(tc, tab, offs, wx, wy, w4_words, w
             codes, scale = h_mx[run]
             for pair in range(2):
                 acc = psum.tile([P, 2, count], F32, name="bank%d" % ((2 * run + pair) % PACK))
-                for i in range(2):
-                    c = 2 * pair + i
+                for side in range(2):
+                    c = 2 * pair + side
                     nc.tensor.matmul_mx(
-                        out=acc[:, i, :],
+                        out=acc[:, side, :],
                         lhsT=w4[:, 2 * P * c: 2 * P * (c + 1)].bitcast(FP4X4),
                         lhsT_scale=w4_scale[:, P * c: P * (c + 1)],
                         rhs=codes[:].bitcast(FP8X4),
@@ -260,12 +267,13 @@ def tile_list_face_gradient_magnitudes_kernel(tc, tab, offs, wx, wy, w4_words, w
                         stop=True,
                     )
                 res = held([P, 2, count], F32, "res%d_%d" % (run, pair))
-                for i in range(2):
-                    column = bias_sb[:, 2 * pair + i: 2 * pair + i + 1]
-                    if run >= len(RUNS) - 2 and pair == 1:
-                        nc.scalar.activation(res[:, i, :], acc[:, i, :], ACT.Identity, bias=column)
-                    else:
-                        nc.vector.tensor_scalar_add(res[:, i, :], acc[:, i, :], column)
+                columns = bias_sb[:, 2 * pair: 2 * pair + 2]
+                if run >= len(RUNS) - SHARED_RUNS and pair == 1:
+                    for side in range(2):
+                        column = columns[:, side: side + 1]
+                        nc.scalar.activation(res[:, side, :], acc[:, side, :], ACT.Identity, bias=column)
+                else:
+                    nc.vector.tensor_add(res[:], acc[:], columns.unsqueeze(2).to_broadcast([P, 2, count]))
                 nc.sync.dma_start(out_tiles[:, 2 * pair: 2 * pair + 2, first: first + count], res[:])
 
         for step in range(len(RUNS) + 2):

from contextlib import ExitStack

import concourse.mybir as mybir

K, T, S, H, N = 2048, 2048, 1024, 512, 512
FLOPS = 2 * 2 * K * H * S + 2 * H * N * S

F32 = mybir.dt.float32
BF16 = mybir.dt.bfloat16
I32 = mybir.dt.int32
U32 = mybir.dt.uint32
U16 = mybir.dt.uint16
U8 = mybir.dt.uint8
FP8X4 = mybir.dt.float8_e4m3fn_x4
FP4X4 = mybir.dt.float4_e2m1fn_x4
ACT = mybir.ActivationFunctionType

P = 128
PACK = 4
K_PASS = P * PACK
PASSES = K // K_PASS
HALF = 512
HALVES = S // HALF
LIST_ROWS = 16

RUNS = ((0, 256), (256, 256), (512, 256), (768, 128), (896, 128))

SHARED_RUNS = 2

SCALAR_PAIRS_X = (2, 2, 1, 1)

MOVED_ROWS = 108

SLOT = 8192
PLACE = {
    "words0": 0,
    "raw_x0": SLOT,
    "gate": 2 * SLOT,
    "raw_x1": 2 * SLOT,
    "words1": 3 * SLOT,
    "raw_x2": 4 * SLOT,
    "rounded_x0": 5 * SLOT,
    "raw_x3": 5 * SLOT,
    "raw_y0": 2 * SLOT,
    "raw_y1": 3 * SLOT,
    "raw_y2": 4 * SLOT,
    "raw_y3_low": 5 * SLOT,
    "raw_y3_high": 5 * SLOT + SLOT // 2,
    "w4": 2 * SLOT,
    "w4_scale": 2 * SLOT + SLOT // 4,
    "bias_sb": 2 * SLOT + SLOT // 2,
}


def tile_list_face_gradient_magnitudes_kernel(tc, tab, offs, wx, wy, w4_words, w4_scales, bias, out):
    nc = tc.nc
    with ExitStack() as ctx:
        keep = ctx.enter_context(tc.tile_pool(name="keep", bufs=1))
        loaded = ctx.enter_context(tc.tile_pool(name="loaded", bufs=1))
        ring = ctx.enter_context(tc.tile_pool(name="ring", bufs=PASSES))
        psum = ctx.enter_context(tc.psum_pool(name="psum", bufs=1))

        def held(shape, dtype, name, tag=None):
            return keep.tile(shape, dtype, name=name, tag=tag or name, align_bytes=64)

        def placed(shape, dtype, name):
            return loaded.tile(shape, dtype, name=name, offset=PLACE[name], align_bytes=64)

        offsets = keep.tile([P, S // LIST_ROWS], U16, name="offsets")
        nc.sync.dma_start(offsets[:], offs)

        tab_scale = held([P, T], U8, "tab_scale")
        nc.vector.memset(tab_scale[:].bitcast(I32), 0)
        gate = placed([P, 3 * SLOT // 4], F32, "gate")
        nc.vector.memset(gate[:, 0:1], 0.0)
        moved_scale = [held([P, S], U8, "moved_scale%d" % a) for a in range(1, PASSES)]
        for tile in moved_scale:
            nc.vector.memset(tile[:].bitcast(I32), 0)

        scale_rows = tab[:, K_PASS * T:].rearrange("d (w Q b vertex) -> d b Q w vertex", w=2, Q=4, b=4)
        for b in range(4):
            for d in range(2):
                queue = nc.gpsimd if b == 3 else nc.scalar
                queue.dma_start(tab_scale[4 * d + b: P: 16, :].bitcast(I32), scale_rows[d, b].bitcast(I32))

        zero = held([P, 1], F32, "zero", "rounded_last")
        nc.scalar.activation(zero[:], gate[:, 0:1], ACT.Sqrt)

        def load_words(d):
            tile = placed([P, T], I32, "words%d" % d)
            nc.sync.dma_start(tile[:], tab[d, : K_PASS * T].rearrange("(p x) -> p x", p=P).bitcast(I32))
            return tile

        def load_weight(weight, a, cols, name):
            rows = weight[a * K_PASS: (a + 1) * K_PASS, cols]
            tile = placed([P, PACK, rows.shape[1]], F32, name)
            nc.sync.dma_start(tile[:], rows.rearrange("(p i) x -> p i x", i=PACK))
            return tile

        def move_scale(a):
            d, w = divmod(a, 2)
            shift = 16 * w + 4 * d
            nc.sync.dma_start(
                moved_scale[a - 1][0:MOVED_ROWS, :].bitcast(I32),
                picked_scale[shift: shift + MOVED_ROWS, :].bitcast(I32),
            )

        def gather_words(d):
            picked = [held([P, HALF], U32, "picked%d_%d" % (d, hf)) for hf in range(HALVES)]
            for hf in range(HALVES):
                entries = offsets[:, hf * HALF // LIST_ROWS: (hf + 1) * HALF // LIST_ROWS]
                nc.vector.tensor_copy(picked[hf][:], words[d][:].bitcast(U32).indirect(entries))
            for hf in range(HALVES):
                parted = held([P, 2, HALF], U16, "parted%d_%d" % (d, hf))
                nc.vector.tensor_copy(parted[:], picked[hf][:].bitcast(U16).rearrange("p (j w) -> p w j", w=2))
                for w in range(2):
                    table[2 * d + w, hf] = parted[:, w, :]

        def round_weight(copy, rounded, raw, pairs, base=0):
            groups = raw.shape[2] // (2 * PACK)
            dst = rounded[:].rearrange("p (u e g f i) -> p u g i f e", u=2, e=2, f=2, i=PACK)
            src = raw[:].rearrange("p i (g f u e) -> p u g i f e", f=2, u=2, e=2)
            for u in pairs:
                copy(dst[:, u, base // 2: base // 2 + groups], src[:, u])

        def round_x(rounded, a):
            round_weight(nc.scalar.copy, rounded, raw_x[a], range(SCALAR_PAIRS_X[a]))
            round_weight(nc.vector.tensor_copy, rounded, raw_x[a], range(SCALAR_PAIRS_X[a], 2))

        def quantise(rounded, name, pieces=1):
            columns = rounded.shape[1] // PACK
            codes = held([P, columns], U32, name + "_codes")
            scale = held([P, columns], U8, name + "_scale")
            width = columns // pieces
            for c0 in range(0, columns, width):
                nc.vector.quantize_mx(
                    out=codes[:, c0: c0 + width].bitcast(FP8X4),
                    scales=scale[:, c0: c0 + width],
                    in_=rounded[:, PACK * c0: PACK * (c0 + width)],
                )
            return codes, scale

        def banks(hf):
            return [psum.tile([P, HALF], F32, name="bank%d" % (PACK * hf + t)) for t in range(PACK)]

        def multiply(acc, weight_mx, a, hf, start, stop, tiles=range(PACK)):
            codes, scale = weight_mx
            for t in tiles:
                cols = slice(t * P, (t + 1) * P)
                nc.tensor.matmul_mx(
                    out=acc[t][:],
                    lhsT=codes[:, cols].bitcast(FP8X4),
                    lhsT_scale=scale[:, cols],
                    rhs=table[a, hf].bitcast(FP4X4),
                    rhs_scale=table_scale[a][:, hf * HALF: (hf + 1) * HALF],
                    start=start,
                    stop=stop,
                )

        whole = slice(0, H)
        words = [load_words(0)]
        raw_x = [load_weight(wx, 0, whole, "raw_x0"), load_weight(wx, 1, whole, "raw_x1")]
        words.append(load_words(1))
        raw_x.append(load_weight(wx, 2, whole, "raw_x2"))

        picked_scale = held([P, S], U8, "picked_scale")
        nc.vector.tensor_copy(picked_scale[:], tab_scale[:].indirect(offsets[:]))
        table_scale = [picked_scale] + moved_scale
        table = {}

        rounded = placed([P, PACK * H], BF16, "rounded_x0")
        round_x(rounded, 0)
        gather_words(0)
        wx_mx = [quantise(rounded, "wx0", pieces=2)]

        move_scale(1)
        raw_x.append(load_weight(wx, 3, whole, "raw_x3"))
        move_scale(2)
        move_scale(3)
        raw_y = [load_weight(wy, a, whole, "raw_y%d" % a) for a in range(PASSES - 1)]
        raw_y_low = load_weight(wy, PASSES - 1, slice(0, H // 2), "raw_y3_low")
        raw_y_high = load_weight(wy, PASSES - 1, slice(H // 2, H), "raw_y3_high")

        w4 = placed([P, 2 * N], U8, "w4")
        nc.sync.dma_start(w4[:].bitcast(I32), w4_words[0].bitcast(I32))
        w4_scale = placed([P, N], U8, "w4_scale")
        nc.vector.memset(w4_scale[:].bitcast(I32), 0)
        for Q in range(4):
            nc.sync.dma_start(
                w4_scale[32 * Q: 32 * Q + 4, :].bitcast(I32), w4_scales[0, 4 * Q: 4 * Q + 4, :].bitcast(I32)
            )
        bias_sb = placed([P, N // P], F32, "bias_sb")
        with nc.allow_non_contiguous_dma(reason="one bias value for each partition and output tile"):
            nc.sync.dma_start(bias_sb[:], bias.rearrange("(c p) -> p c", p=P))

        gx = [banks(hf) for hf in range(HALVES)]
        for a in range(PASSES):
            if a > 0:
                rounded = ring.tile([P, PACK * H], BF16, name="rounded", align_bytes=64)
                round_x(rounded, a)
                if a % 2 == 0:
                    gather_words(a // 2)
                wx_mx.append(quantise(rounded, "wx%d" % a, pieces=2))
            for hf in range(HALVES):
                multiply(gx[hf], wx_mx[a], a, hf, start=(a == 0), stop=(a == PASSES - 1))

        gx2 = [held([P, PACK, HALF], F32, "gx2_%d" % hf) for hf in range(HALVES)]
        for hf in range(HALVES):
            for t in range(PACK):
                nc.scalar.activation(gx2[hf][:, t, :], gx[hf][t][:], ACT.Square, bias=zero[:])

        wy_mx = []
        for a in range(PASSES - 1):
            rounded = ring.tile([P, PACK * H], BF16, name="rounded", align_bytes=64)
            round_weight(nc.vector.tensor_copy, rounded, raw_y[a], range(2))
            wy_mx.append(quantise(rounded, "wy%d" % a, pieces=2))
        rounded = held([P, PACK * H], BF16, "rounded_last")
        round_weight(nc.scalar.copy, rounded, raw_y_low, range(2))
        round_weight(nc.vector.tensor_copy, rounded, raw_y_high, range(2), base=P // 2)
        wy_mx.append(quantise(rounded, "wy3", pieces=PACK))

        gy = [banks(hf) for hf in range(HALVES)]
        for a in range(PASSES):
            multiply(gy[0], wy_mx[a], a, 0, start=(a == 0), stop=(a == PASSES - 1))
        for a in (0, 3):
            multiply(gy[1], wy_mx[a], a, 1, start=(a == 0), stop=False)
        for t in range(PACK):
            for a in (1, 2):
                multiply(gy[1], wy_mx[a], a, 1, start=False, stop=(a == 2), tiles=(t,))

        out_tiles = out.rearrange("(c p) j -> p c j", p=P)
        sums, h_mx = {}, {}

        def square_and_add(run):
            first, count = RUNS[run]
            hf = first // HALF
            cols = slice(first % HALF, first % HALF + count)
            gy2 = held([P, PACK, count], F32, "gy2_%d" % run)
            for t in range(PACK):
                nc.scalar.activation(gy2[:, t, :], gy[hf][t][:, cols], ACT.Square)
            sums[run] = held([P, PACK, count], F32, "sum%d" % run)
            nc.vector.tensor_add(sums[run][:], gy2[:], gx2[hf][:, :, cols])

        def root(run):
            h = held([P, PACK * RUNS[run][1]], BF16, "h%d" % run)
            nc.scalar.activation(
                h[:].rearrange("p (four j t) -> p four t j", j=4, t=PACK),
                sums[run][:].rearrange("p t (four j) -> p four t j", j=4),
                ACT.Sqrt,
            )
            h_mx[run] = quantise(h, "h%d" % run)

        def project(run):
            first, count = RUNS[run]
            codes, scale = h_mx[run]
            for pair in range(2):
                acc = psum.tile([P, 2, count], F32, name="bank%d" % ((2 * run + pair) % PACK))
                for side in range(2):
                    c = 2 * pair + side
                    nc.tensor.matmul_mx(
                        out=acc[:, side, :],
                        lhsT=w4[:, 2 * P * c: 2 * P * (c + 1)].bitcast(FP4X4),
                        lhsT_scale=w4_scale[:, P * c: P * (c + 1)],
                        rhs=codes[:].bitcast(FP8X4),
                        rhs_scale=scale[:],
                        start=True,
                        stop=True,
                    )
                res = held([P, 2, count], F32, "res%d_%d" % (run, pair))
                columns = bias_sb[:, 2 * pair: 2 * pair + 2]
                if run >= len(RUNS) - SHARED_RUNS and pair == 1:
                    for side in range(2):
                        column = columns[:, side: side + 1]
                        nc.scalar.activation(res[:, side, :], acc[:, side, :], ACT.Identity, bias=column)
                else:
                    nc.vector.tensor_add(res[:], acc[:], columns.unsqueeze(2).to_broadcast([P, 2, count]))
                nc.sync.dma_start(out_tiles[:, 2 * pair: 2 * pair + 2, first: first + count], res[:])

        for step in range(len(RUNS) + 2):
            if step < len(RUNS):
                square_and_add(step)
            if 1 <= step <= len(RUNS):
                root(step - 1)
            if step >= 2:
                project(step - 2)
